import numpy as np
import ml_dtypes


def mxq(x, axis, fmt="e4m3"):
    dtype, down = {"e4m3": (ml_dtypes.float8_e4m3fn, 7), "e5m2": (ml_dtypes.float8_e5m2, 14)}[fmt]
    v = np.moveaxis(np.asarray(x, np.float32).astype(ml_dtypes.bfloat16).astype(np.float64), axis, -1)
    blocks = v.reshape(v.shape[:-1] + (-1, 32))
    amax = np.abs(blocks).max(-1, keepdims=True)
    byte = np.maximum(np.where(amax > 0, np.frexp(amax)[1] - 1 + 127, 0) - down, 1)
    scale = np.exp2(byte - 127.0)
    codes = (blocks / scale).astype(np.float32).astype(dtype).astype(np.float64)
    return np.moveaxis((codes * scale).reshape(v.shape), -1, axis)


WIDE = False


def mx_kscale(k):
    if not WIDE:
        return np.ones(k)
    levels = np.array([10, -10, 5, -5, 0])
    if k % 512:
        return np.exp2(np.random.permutation(np.resize(levels, k // 32))).repeat(32)
    a = np.empty((k // 512, 16))
    for p in range(k // 512):
        a[p, :8] = np.random.permutation(np.resize(levels, 8))
        for g in range(8):
            far = levels[np.abs(levels - a[p, g]) >= 10]
            a[p, g + 8] = far[np.random.randint(len(far))]
    return np.exp2(a.ravel()).repeat(32)


def f64(x):
    return np.asarray(x).astype(np.float64)


def striped8(idx):
    return np.concatenate([v.reshape(-1, 16).T for v in idx]).astype(np.uint16)


def unstriped8(offs):
    return np.stack([offs[16 * g:16 * g + 16].T.reshape(-1) for g in range(8)]).astype(np.int64)


E2M1 = np.array([0.0, 0.5, 1.0, 1.5, 2.0, 3.0, 4.0, 6.0, -0.0, -0.5, -1.0, -1.5, -2.0, -3.0, -4.0, -6.0])


def pack_weight(w, fmt):
    k, n = w.shape
    w = f64(np.asarray(w, np.float32).astype(ml_dtypes.bfloat16)).reshape(k // 32, 32, n)
    amax = np.abs(w).max(1)
    if fmt == "e4m3":
        byte = np.frexp(amax)[1] - 1 + 127 - 7
    else:
        mant, ex = np.frexp(amax / 6.0)
        byte = np.where(mant > 0.5, ex, ex - 1) + 127
    byte = np.clip(np.where(amax > 0, byte, 1), 1, 254)
    scaled = (w * np.exp2(127.0 - byte)[:, None, :]).reshape(k, n).astype(np.float32)
    by_word = np.ascontiguousarray(scaled.reshape(k // 512, 128, 4, n).transpose(0, 1, 3, 2))
    if fmt == "e4m3":
        words = by_word.astype(ml_dtypes.float8_e4m3fn).view(np.uint8)
    else:
        c = by_word.astype(ml_dtypes.float4_e2m1fn).view(np.uint8) & 0xF
        words = (c[..., 0::2] | (c[..., 1::2] << 4)).reshape(k // 512, 128, 2 * n)
    return np.ascontiguousarray(words), np.ascontiguousarray(byte.astype(np.uint8).reshape(k // 512, 16, n))


def unpack_weight(words, scales, fmt):
    g, _, n = scales.shape
    words = np.ascontiguousarray(words).reshape(g, 128, n, -1)
    if fmt == "e4m3":
        vals = words.view(ml_dtypes.float8_e4m3fn).astype(np.float64)
    else:
        nib = np.empty((g, 128, n, 4), np.uint8)
        nib[..., 0::2] = words & 0xF
        nib[..., 1::2] = words >> 4
        vals = E2M1[nib]
    vals = vals * np.repeat(np.exp2(scales.astype(np.float64) - 127.0), 8, axis=1)[..., None]
    return vals.transpose(0, 1, 3, 2).reshape(g * 512, n)


K, R, M, T, S = 1024, 512, 1536, 1024, 512


def setup_inputs():
    n = np.random.standard_normal
    s = mx_kscale(K)[:, None]
    u = mx_kscale(R)[:, None]
    p_w4 = pack_weight(n((K, M)) / np.sqrt(K) / s, "e2m1")
    return {
        "xT": (n((K, T)) * s).astype(np.float32),
        "w4_words": p_w4[0],
        "w4_scales": p_w4[1],
        "down": (n((K, R)) / np.sqrt(K) / s * u.T).astype(np.float32),
        "up": (0.5 * n((R, M)) / np.sqrt(R) / u).astype(np.float32),
        "wgt": np.repeat(np.random.uniform(0.5, 2.0, (8, S)), 16, axis=0).astype(np.float32),
        "prev": (n((512, 1536))).astype(np.float32),
        "offs": striped8(np.stack([np.random.permutation(T)[:S] for _ in range(8)])),
    }


def reference(xT, w4_words, w4_scales, down, up, wgt, prev, offs):
    idx = unstriped8(offs)
    group = np.arange(K) % 512 // 64
    xg = f64(wgt)[np.arange(K) // 4 % 128] * f64(xT)[np.arange(K)[:, None], idx[group]]
    xT_ = mxq(xg, 0, "e4m3")
    w4_ = unpack_weight(w4_words, w4_scales, "e2m1")
    down_ = mxq(f64(down), 0, "e4m3")
    up_ = mxq(f64(up), 0, "e4m3")
    h_ = mxq(down_.T @ xT_, 0, "e4m3")
    y = xT_.T @ w4_ + h_.T @ up_
    return f64(prev) + y

@@ -1,0 +1,208 @@
+from contextlib import ExitStack
+
+import concourse.mybir as mybir
+
+K, R, M, T, S = 1024, 512, 1536, 1024, 512
+FLOPS = 2 * S * (K * R + K * M + R * M)
+
+F32 = mybir.dt.float32
+BF16 = mybir.dt.bfloat16
+I32 = mybir.dt.int32
+U32 = mybir.dt.uint32
+U16 = mybir.dt.uint16
+U8 = mybir.dt.uint8
+E4M3 = mybir.dt.float8_e4m3fn_x4
+E2M1 = mybir.dt.float4_e2m1fn_x4
+MULT = mybir.AluOpType.mult
+
+P = 128
+PASSES = K // 512
+HALF = S // 2
+NC = 512
+CHUNKS = M // NC
+JT = S // P
+
+
+def interleave(copy, out, in_):
+    copy(out=out.rearrange("p (c i) t -> p c t i", i=4), in_=in_.rearrange("p t (c i) -> p c t i", i=4))
+
+
+def tile_list_hlora_tm_res_kernel(tc, xT, w4_words, w4_scales, down, up, wgt, prev, offs, out):
+    nc = tc.nc
+    scopy = nc.scalar.copy
+    vcopy = nc.vector.tensor_copy
+    with ExitStack() as ctx:
+        sb = ctx.enter_context(tc.tile_pool(name="sb", bufs=1))
+        ps = ctx.enter_context(tc.psum_pool(name="ps", bufs=8))
+
+        lists = sb.tile([P, S // 16], U16, name="lists")
+        nc.sync.dma_start(lists[:], offs)
+        w4s = sb.tile([P, PASSES, M], U8, name="w4s", align_bytes=64)
+        nc.gpsimd.memset(w4s[:].bitcast(I32), 0)
+        for q in range(4):
+            nc.gpsimd.dma_start(
+                out=w4s[32 * q : 32 * q + 4, :, :].bitcast(I32),
+                in_=w4_scales[:, 4 * q : 4 * q + 4, :].bitcast(I32).rearrange("a q n -> q a n"),
+            )
+        planes = {}
+        wg = sb.tile([P, S], F32, name="wg")
+        for a in range(PASSES):
+            rows = xT[512 * a : 512 * (a + 1), :].rearrange("(p i) t -> p i t", i=4)
+            for i in range(4):
+                planes[a, i] = sb.tile([P, T], F32, name=f"x{a}{i}")
+                nc.sync.dma_start(out=planes[a, i][:], in_=rows[:, i, :])
+                if a == 0 and i == 0:
+                    nc.sync.dma_start(out=wg[:], in_=wgt)
+        w4 = sb.tile([P, PASSES, 2 * M], U8, name="w4", align_bytes=64)
+        nc.sync.dma_start(out=w4[:].bitcast(I32), in_=w4_words.bitcast(I32).rearrange("a p n -> p a n"))
+        draw = []
+        for a in range(PASSES):
+            d = sb.tile([P, 4, R], F32, name=f"draw{a}")
+            nc.sync.dma_start(out=d[:], in_=down[512 * a : 512 * (a + 1), :].rearrange("(p j) r -> p j r", j=4))
+            draw.append(d)
+        uraw = []
+        for c in range(CHUNKS):
+            u = sb.tile([P, 4, NC], F32, name=f"uraw{c}")
+            nc.sync.dma_start(out=u[:], in_=up[:, NC * c : NC * (c + 1)].rearrange("(p j) n -> p j n", j=4))
+            uraw.append(u)
+        pv = []
+        for j in range(JT):
+            t = sb.tile([P, M], F32, name=f"prev{j}")
+            nc.sync.dma_start(out=t[:], in_=prev[P * j : P * (j + 1), :])
+            pv.append(t)
+
+        xc, xs, gath, xb = {}, {}, {}, {}
+        for a in range(PASSES):
+            xc[a] = sb.tile([P, S], U32, name=f"xc{a}", align_bytes=64)
+            xs[a] = sb.tile([P, S], U8, name=f"xs{a}", align_bytes=64)
+            for h in range(2):
+                gath[a, h] = sb.tile([P, 4, HALF], F32, name=f"g{a}{h}")
+                xb[a, h] = sb.tile([P, HALF, 4], BF16, name=f"xb{a}{h}", align_bytes=64)
+
+        def gather(a, i):
+            for h in range(2):
+                nc.vector.tensor_tensor(
+                    gath[a, h][:, i, :],
+                    planes[a, i][:].indirect(lists[:, h * HALF // 16 : (h + 1) * HALF // 16]),
+                    wg[:, h * HALF : (h + 1) * HALF],
+                    MULT,
+                )
+
+        def quantize_x(a, h):
+            cols = slice(h * HALF, (h + 1) * HALF)
+            nc.vector.quantize_mx(
+                out=xc[a][:, cols].bitcast(E4M3), scales=xs[a][:, cols], in_=xb[a, h][:].rearrange("p j t -> p (j t)")
+            )
+
+        for i in range(4):
+            gather(0, i)
+        for h in range(2):
+            interleave(scopy, xb[0, h][:], gath[0, h][:])
+        gather(1, 0)
+        gather(1, 1)
+        quantize_x(0, 0)
+        gather(1, 2)
+        quantize_x(0, 1)
+        gather(1, 3)
+        interleave(scopy, xb[1, 0][:], gath[1, 0][:])
+        interleave(vcopy, xb[1, 1][:], gath[1, 1][:])
+
+        dc, ds = {}, {}
+
+        def cast_down(copy, a):
+            b = sb.tile([P, R, 4], BF16, name=f"db{a}", align_bytes=64)
+            copy(
+                out=b[:].rearrange("p (t m) j -> p m t j", t=4),
+                in_=draw[a][:].rearrange("p j (m t) -> p m t j", t=4),
+            )
+            return b
+
+        def quantize_down(a, b):
+            dc[a] = sb.tile([P, R], U32, name=f"dc{a}", align_bytes=64)
+            ds[a] = sb.tile([P, R], U8, name=f"ds{a}", align_bytes=64)
+            nc.vector.quantize_mx(out=dc[a][:].bitcast(E4M3), scales=ds[a][:], in_=b[:].rearrange("p r j -> p (r j)"))
+
+        d0 = cast_down(scopy, 0)
+        d1 = cast_down(vcopy, 1)
+        quantize_x(1, 0)
+        quantize_x(1, 1)
+        quantize_down(0, d0)
+        quantize_down(1, d1)
+
+        acc = {}
+
+        def base(j, c):
+            acc[j, c] = ps.tile([P, NC], F32, name=f"acc{j}{c}", tag="bank")
+            for a in range(PASSES):
+                nc.tensor.matmul_mx(
+                    out=acc[j, c][:],
+                    lhsT=xc[a][:, P * j : P * (j + 1)].bitcast(E4M3),
+                    lhsT_scale=xs[a][:, P * j : P * (j + 1)],
+                    rhs=w4[:, a, 2 * NC * c : 2 * NC * (c + 1)].bitcast(E2M1),
+                    rhs_scale=w4s[:, a, NC * c : NC * (c + 1)],
+                    start=(a == 0),
+                    stop=False,
+                )
+
+        for j in range(2):
+            for c in range(CHUNKS):
+                base(j, c)
+
+        hc = sb.tile([P, S], U32, name="hc", align_bytes=64)
+        hs = sb.tile([P, S], U8, name="hs", align_bytes=64)
+        for j in range(JT):
+            cols = slice(P * j, P * (j + 1))
+            bank = ps.tile([P, 4, P], F32, name=f"h{j}", tag="bank")
+            for t in range(4):
+                for a in range(PASSES):
+                    nc.tensor.matmul_mx(
+                        out=bank[:, t, :],
+                        lhsT=dc[a][:, P * t : P * (t + 1)].bitcast(E4M3),
+                        lhsT_scale=ds[a][:, P * t : P * (t + 1)],
+                        rhs=xc[a][:, cols].bitcast(E4M3),
+                        rhs_scale=xs[a][:, cols],
+                        start=(a == 0),
+                        stop=(a == PASSES - 1),
+                    )
+            hb = sb.tile([P, P, 4], BF16, name=f"hb{j}", align_bytes=64)
+            copy = scopy if j % 2 == 0 else vcopy
+            copy(out=hb[:], in_=bank[:].rearrange("p t j -> p j t"))
+            nc.vector.quantize_mx(
+                out=hc[:, cols].bitcast(E4M3), scales=hs[:, cols], in_=hb[:].rearrange("p j t -> p (j t)")
+            )
+
+        ub, uc, us = [], [], []
+        for c in range(CHUNKS):
+            ub.append(sb.tile([P, NC, 4], BF16, name=f"ub{c}", align_bytes=64))
+            uc.append(sb.tile([P, NC], U32, name=f"uc{c}", align_bytes=64))
+            us.append(sb.tile([P, NC], U8, name=f"us{c}", align_bytes=64))
+
+        def quantize_up(c):
+            nc.vector.quantize_mx(out=uc[c][:].bitcast(E4M3), scales=us[c][:], in_=ub[c][:].rearrange("p n j -> p (n j)"))
+
+        interleave(scopy, ub[0][:], uraw[0][:])
+        interleave(vcopy, ub[1][:], uraw[1][:])
+        quantize_up(0)
+        interleave(scopy, ub[2][:, :256, :], uraw[2][:, :, :256])
+        interleave(vcopy, ub[2][:, 256:, :], uraw[2][:, :, 256:])
+        quantize_up(1)
+        quantize_up(2)
+
+        for j in range(JT):
+            for c in range(CHUNKS):
+                if j >= 2:
+                    base(j, c)
+            res = sb.tile([P, M], F32, name=f"res{j}")
+            for c in range(CHUNKS):
+                nc.tensor.matmul_mx(
+                    out=acc[j, c][:],
+                    lhsT=hc[:, P * j : P * (j + 1)].bitcast(E4M3),
+                    lhsT_scale=hs[:, P * j : P * (j + 1)],
+                    rhs=uc[c][:].bitcast(E4M3),
+                    rhs_scale=us[c][:],
+                    start=False,
+                    stop=True,
+                )
+                ncols = slice(NC * c, NC * (c + 1))
+                nc.vector.tensor_add(out=res[:, ncols], in0=acc[j, c][:], in1=pv[j][:, ncols])
+            nc.sync.dma_start(out=out[P * j : P * (j + 1), :], in_=res[:])

@@ -36,40 +36,46 @@ def tile_list_hlora_tm_res_kernel(tc, xT, w4_words, w4_scales, down, up, wgt, pr
         ps = ctx.enter_context(tc.psum_pool(name="ps", bufs=8))
 
         lists = sb.tile([P, S // 16], U16, name="lists")
-        nc.sync.dma_start(lists[:], offs)
         w4s = sb.tile([P, PASSES, M], U8, name="w4s", align_bytes=64)
-        nc.gpsimd.memset(w4s[:].bitcast(I32), 0)
+        nc.vector.memset(w4s[:].bitcast(I32), 0)
+        w4 = sb.tile([P, PASSES, 2 * M], U8, name="w4", align_bytes=64)
+        wg = sb.tile([P, S], F32, name="wg")
+        planes, draw, uraw, pv = {}, {}, {}, {}
+
+        def load_x(a, i):
+            planes[a, i] = sb.tile([P, T], F32, name=f"x{a}{i}")
+            rows = xT[512 * a : 512 * (a + 1), :].rearrange("(p i) t -> p i t", i=4)
+            nc.sync.dma_start(out=planes[a, i][:], in_=rows[:, i, :])
+
+        def load_down(a):
+            draw[a] = sb.tile([P, 4, R], F32, name=f"draw{a}")
+            nc.sync.dma_start(out=draw[a][:], in_=down[512 * a : 512 * (a + 1), :].rearrange("(p j) r -> p j r", j=4))
+
+        def load_up(c):
+            uraw[c] = sb.tile([P, 4, NC], F32, name=f"uraw{c}")
+            nc.sync.dma_start(out=uraw[c][:], in_=up[:, NC * c : NC * (c + 1)].rearrange("(p j) n -> p j n", j=4))
+
+        nc.sync.dma_start(lists[:], offs)
+        load_x(0, 0)
+        nc.sync.dma_start(out=wg[:], in_=wgt)
         for q in range(4):
-            nc.gpsimd.dma_start(
+            nc.sync.dma_start(
                 out=w4s[32 * q : 32 * q + 4, :, :].bitcast(I32),
                 in_=w4_scales[:, 4 * q : 4 * q + 4, :].bitcast(I32).rearrange("a q n -> q a n"),
             )
-        planes = {}
-        wg = sb.tile([P, S], F32, name="wg")
-        for a in range(PASSES):
-            rows = xT[512 * a : 512 * (a + 1), :].rearrange("(p i) t -> p i t", i=4)
-            for i in range(4):
-                planes[a, i] = sb.tile([P, T], F32, name=f"x{a}{i}")
-                nc.sync.dma_start(out=planes[a, i][:], in_=rows[:, i, :])
-                if a == 0 and i == 0:
-                    nc.sync.dma_start(out=wg[:], in_=wgt)
-        w4 = sb.tile([P, PASSES, 2 * M], U8, name="w4", align_bytes=64)
+        for i in range(1, 4):
+            load_x(0, i)
+        for i in range(4):
+            load_x(1, i)
         nc.sync.dma_start(out=w4[:].bitcast(I32), in_=w4_words.bitcast(I32).rearrange("a p n -> p a n"))
-        draw = []
-        for a in range(PASSES):
-            d = sb.tile([P, 4, R], F32, name=f"draw{a}")
-            nc.sync.dma_start(out=d[:], in_=down[512 * a : 512 * (a + 1), :].rearrange("(p j) r -> p j r", j=4))
-            draw.append(d)
-        uraw = []
-        for c in range(CHUNKS):
-            u = sb.tile([P, 4, NC], F32, name=f"uraw{c}")
-            nc.sync.dma_start(out=u[:], in_=up[:, NC * c : NC * (c + 1)].rearrange("(p j) n -> p j n", j=4))
-            uraw.append(u)
-        pv = []
+        load_down(0)
+        load_down(1)
+        load_up(0)
+        load_up(1)
+        load_up(2)
         for j in range(JT):
-            t = sb.tile([P, M], F32, name=f"prev{j}")
-            nc.sync.dma_start(out=t[:], in_=prev[P * j : P * (j + 1), :])
-            pv.append(t)
+            pv[j] = sb.tile([P, M], F32, name=f"prev{j}")
+            nc.sync.dma_start(out=pv[j][:], in_=prev[P * j : P * (j + 1), :])
 
         xc, xs, gath, xb = {}, {}, {}, {}
         for a in range(PASSES):
@@ -79,14 +85,13 @@ def tile_list_hlora_tm_res_kernel(tc, xT, w4_words, w4_scales, down, up, wgt, pr
                 gath[a, h] = sb.tile([P, 4, HALF], F32, name=f"g{a}{h}")
                 xb[a, h] = sb.tile([P, HALF, 4], BF16, name=f"xb{a}{h}", align_bytes=64)
 
-        def gather(a, i):
-            for h in range(2):
-                nc.vector.tensor_tensor(
-                    gath[a, h][:, i, :],
-                    planes[a, i][:].indirect(lists[:, h * HALF // 16 : (h + 1) * HALF // 16]),
-                    wg[:, h * HALF : (h + 1) * HALF],
-                    MULT,
-                )
+        def gather(a, i, h):
+            nc.vector.tensor_tensor(
+                gath[a, h][:, i, :],
+                planes[a, i][:].indirect(lists[:, h * HALF // 16 : (h + 1) * HALF // 16]),
+                wg[:, h * HALF : (h + 1) * HALF],
+                MULT,
+            )
 
         def quantize_x(a, h):
             cols = slice(h * HALF, (h + 1) * HALF)
@@ -94,40 +99,53 @@ def tile_list_hlora_tm_res_kernel(tc, xT, w4_words, w4_scales, down, up, wgt, pr
                 out=xc[a][:, cols].bitcast(E4M3), scales=xs[a][:, cols], in_=xb[a, h][:].rearrange("p j t -> p (j t)")
             )
 
-        for i in range(4):
-            gather(0, i)
-        for h in range(2):
-            interleave(scopy, xb[0, h][:], gath[0, h][:])
-        gather(1, 0)
-        gather(1, 1)
-        quantize_x(0, 0)
-        gather(1, 2)
-        quantize_x(0, 1)
-        gather(1, 3)
-        interleave(scopy, xb[1, 0][:], gath[1, 0][:])
-        interleave(vcopy, xb[1, 1][:], gath[1, 1][:])
-
-        dc, ds = {}, {}
-
-        def cast_down(copy, a):
-            b = sb.tile([P, R, 4], BF16, name=f"db{a}", align_bytes=64)
-            copy(
-                out=b[:].rearrange("p (t m) j -> p m t j", t=4),
-                in_=draw[a][:].rearrange("p j (m t) -> p m t j", t=4),
-            )
-            return b
-
-        def quantize_down(a, b):
+        dc, ds, db = {}, {}, {}
+        for a in range(PASSES):
+            db[a] = sb.tile([P, R, 4], BF16, name=f"db{a}", align_bytes=64)
             dc[a] = sb.tile([P, R], U32, name=f"dc{a}", align_bytes=64)
             ds[a] = sb.tile([P, R], U8, name=f"ds{a}", align_bytes=64)
-            nc.vector.quantize_mx(out=dc[a][:].bitcast(E4M3), scales=ds[a][:], in_=b[:].rearrange("p r j -> p (r j)"))
 
-        d0 = cast_down(scopy, 0)
-        d1 = cast_down(vcopy, 1)
+        def cast_down(copy, a, lo, hi):
+            copy(
+                out=db[a][:].rearrange("p (t m) j -> p m t j", t=4)[:, lo:hi],
+                in_=draw[a][:].rearrange("p j (m t) -> p m t j", t=4)[:, lo:hi],
+            )
+
+        def quantize_down(a):
+            nc.vector.quantize_mx(
+                out=dc[a][:].bitcast(E4M3), scales=ds[a][:], in_=db[a][:].rearrange("p r j -> p (r j)")
+            )
+
+        ub, uc, us = [], [], []
+        for c in range(CHUNKS):
+            ub.append(sb.tile([P, NC, 4], BF16, name=f"ub{c}", align_bytes=64))
+            uc.append(sb.tile([P, NC], U32, name=f"uc{c}", align_bytes=64))
+            us.append(sb.tile([P, NC], U8, name=f"us{c}", align_bytes=64))
+
+        def cast_up(copy, c, lo, hi):
+            interleave(copy, ub[c][:, lo:hi, :], uraw[c][:, :, lo:hi])
+
+        def quantize_up(c):
+            nc.vector.quantize_mx(out=uc[c][:].bitcast(E4M3), scales=us[c][:], in_=ub[c][:].rearrange("p n j -> p (n j)"))
+
+        for i in range(4):
+            for h in range(2):
+                gather(0, i, h)
+        for h in range(2):
+            interleave(scopy, xb[0, h][:], gath[0, h][:])
+        for i in range(4):
+            for h in range(2):
+                gather(1, i, h)
+            if i in (1, 2):
+                quantize_x(0, i - 1)
+        interleave(scopy, xb[1, 0][:], gath[1, 0][:])
+        interleave(vcopy, xb[1, 1][:], gath[1, 1][:])
+        cast_down(scopy, 0, 0, P)
+        cast_down(vcopy, 1, 0, P)
         quantize_x(1, 0)
         quantize_x(1, 1)
-        quantize_down(0, d0)
-        quantize_down(1, d1)
+        quantize_down(0)
+        quantize_down(1)
 
         acc = {}
 
@@ -165,32 +183,24 @@ def tile_list_hlora_tm_res_kernel(tc, xT, w4_words, w4_scales, down, up, wgt, pr
                         stop=(a == PASSES - 1),
                     )
             hb = sb.tile([P, P, 4], BF16, name=f"hb{j}", align_bytes=64)
-            copy = scopy if j % 2 == 0 else vcopy
-            copy(out=hb[:], in_=bank[:].rearrange("p t j -> p j t"))
+            scopy(out=hb[:], in_=bank[:].rearrange("p t j -> p j t"))
             nc.vector.quantize_mx(
                 out=hc[:, cols].bitcast(E4M3), scales=hs[:, cols], in_=hb[:].rearrange("p j t -> p (j t)")
             )
 
-        ub, uc, us = [], [], []
-        for c in range(CHUNKS):
-            ub.append(sb.tile([P, NC, 4], BF16, name=f"ub{c}", align_bytes=64))
-            uc.append(sb.tile([P, NC], U32, name=f"uc{c}", align_bytes=64))
-            us.append(sb.tile([P, NC], U8, name=f"us{c}", align_bytes=64))
-
-        def quantize_up(c):
-            nc.vector.quantize_mx(out=uc[c][:].bitcast(E4M3), scales=us[c][:], in_=ub[c][:].rearrange("p n j -> p (n j)"))
-
-        interleave(scopy, ub[0][:], uraw[0][:])
-        interleave(vcopy, ub[1][:], uraw[1][:])
+        cast_up(scopy, 0, 0, NC)
+        cast_up(vcopy, 1, 0, NC)
         quantize_up(0)
-        interleave(scopy, ub[2][:, :256, :], uraw[2][:, :, :256])
-        interleave(vcopy, ub[2][:, 256:, :], uraw[2][:, :, 256:])
+        cast_up(scopy, 2, 0, NC // 2)
+        cast_up(vcopy, 2, NC // 2, NC)
         quantize_up(1)
         quantize_up(2)
 
+        base(2, 0)
+        base(2, 1)
         for j in range(JT):
             for c in range(CHUNKS):
-                if j >= 2:
+                if (j, c) not in acc:
                     base(j, c)
             res = sb.tile([P, M], F32, name=f"res{j}")
             for c in range(CHUNKS):
@@ -205,4 +215,9 @@ def tile_list_hlora_tm_res_kernel(tc, xT, w4_words, w4_scales, down, up, wgt, pr
                 )
                 ncols = slice(NC * c, NC * (c + 1))
                 nc.vector.tensor_add(out=res[:, ncols], in0=acc[j, c][:], in1=pv[j][:, ncols])
-            nc.sync.dma_start(out=out[P * j : P * (j + 1), :], in_=res[:])
+            rows = out[P * j : P * (j + 1), :]
+            if j < JT - 1:
+                nc.sync.dma_start(out=rows, in_=res[:])
+            else:
+                nc.sync.dma_start(out=rows[:, : 2 * NC], in_=res[:, : 2 * NC])
+                nc.sync.dma_start(out=rows[:, 2 * NC :], in_=res[:, 2 * NC :])

@@ -58,15 +58,15 @@ def tile_list_hlora_tm_res_kernel(tc, xT, w4_words, w4_scales, down, up, wgt, pr
         nc.sync.dma_start(lists[:], offs)
         load_x(0, 0)
         nc.sync.dma_start(out=wg[:], in_=wgt)
-        for q in range(4):
-            nc.sync.dma_start(
-                out=w4s[32 * q : 32 * q + 4, :, :].bitcast(I32),
-                in_=w4_scales[:, 4 * q : 4 * q + 4, :].bitcast(I32).rearrange("a q n -> q a n"),
-            )
         for i in range(1, 4):
             load_x(0, i)
         for i in range(4):
             load_x(1, i)
+        for r in range(4):
+            nc.sync.dma_start(
+                out=w4s[r:P:32, :, :].bitcast(I32),
+                in_=w4_scales.bitcast(I32).rearrange("a (q r) n -> r q a n", r=4)[r],
+            )
         nc.sync.dma_start(out=w4[:].bitcast(I32), in_=w4_words.bitcast(I32).rearrange("a p n -> p a n"))
         load_down(0)
         load_down(1)

@@ -70,9 +70,8 @@ def tile_list_hlora_tm_res_kernel(tc, xT, w4_words, w4_scales, down, up, wgt, pr
         nc.sync.dma_start(out=w4[:].bitcast(I32), in_=w4_words.bitcast(I32).rearrange("a p n -> p a n"))
         load_down(0)
         load_down(1)
-        load_up(0)
-        load_up(1)
-        load_up(2)
+        for c in range(CHUNKS):
+            load_up(c)
         for j in range(JT):
             pv[j] = sb.tile([P, M], F32, name=f"prev{j}")
             nc.sync.dma_start(out=pv[j][:], in_=prev[P * j : P * (j + 1), :])
@@ -198,26 +197,39 @@ def tile_list_hlora_tm_res_kernel(tc, xT, w4_words, w4_scales, down, up, wgt, pr
 
         base(2, 0)
         base(2, 1)
-        for j in range(JT):
-            for c in range(CHUNKS):
-                if (j, c) not in acc:
-                    base(j, c)
+
+        def finish(j, c, res):
+            if (j, c) not in acc:
+                base(j, c)
+            nc.tensor.matmul_mx(
+                out=acc[j, c][:],
+                lhsT=hc[:, P * j : P * (j + 1)].bitcast(E4M3),
+                lhsT_scale=hs[:, P * j : P * (j + 1)],
+                rhs=uc[c][:].bitcast(E4M3),
+                rhs_scale=us[c][:],
+                start=False,
+                stop=True,
+            )
+            residual = pv[j][:, NC * c : NC * (c + 1)]
+            if (j, c) in ((1, 1), (2, 1), (3, 0)):
+                y = sb.tile([P, NC], F32, name=f"y{j}")
+                scopy(out=y[:], in_=acc[j, c][:])
+                nc.gpsimd.tensor_tensor(out=res, in0=y[:], in1=residual, op=mybir.AluOpType.add)
+            else:
+                nc.vector.tensor_add(out=res, in0=acc[j, c][:], in1=residual)
+
+        SPLIT = 2 * NC
+        for j in range(2):
+            left = sb.tile([P, SPLIT], F32, name=f"left{j}")
+            for c in range(2):
+                finish(j, c, left[:, NC * c : NC * (c + 1)])
+            nc.sync.dma_start(out=out[P * j : P * (j + 1), :SPLIT], in_=left[:])
+        right = sb.tile([P, 2, NC], F32, name="right")
+        for j in range(2):
+            finish(j, 2, right[:, j, :])
+        nc.sync.dma_start(out=out[: 2 * P, SPLIT:].rearrange("(j p) n -> p j n", p=P), in_=right[:])
+        for j in (2, 3):
             res = sb.tile([P, M], F32, name=f"res{j}")
             for c in range(CHUNKS):
-                nc.tensor.matmul_mx(
-                    out=acc[j, c][:],
-                    lhsT=hc[:, P * j : P * (j + 1)].bitcast(E4M3),
-                    lhsT_scale=hs[:, P * j : P * (j + 1)],
-                    rhs=uc[c][:].bitcast(E4M3),
-                    rhs_scale=us[c][:],
-                    start=False,
-                    stop=True,
-                )
-                ncols = slice(NC * c, NC * (c + 1))
-                nc.vector.tensor_add(out=res[:, ncols], in0=acc[j, c][:], in1=pv[j][:, ncols])
-            rows = out[P * j : P * (j + 1), :]
-            if j < JT - 1:
-                nc.sync.dma_start(out=rows, in_=res[:])
-            else:
-                nc.sync.dma_start(out=rows[:, : 2 * NC], in_=res[:, : 2 * NC])
-                nc.sync.dma_start(out=rows[:, 2 * NC :], in_=res[:, 2 * NC :])
+                finish(j, c, res[:, NC * c : NC * (c + 1)])
+            nc.sync.dma_start(out=out[P * j : P * (j + 1), :], in_=res[:])

from contextlib import ExitStack

import concourse.mybir as mybir

K, R, M, T, S = 1024, 512, 1536, 1024, 512
FLOPS = 2 * S * (K * R + K * M + R * M)

F32 = mybir.dt.float32
BF16 = mybir.dt.bfloat16
I32 = mybir.dt.int32
U32 = mybir.dt.uint32
U16 = mybir.dt.uint16
U8 = mybir.dt.uint8
E4M3 = mybir.dt.float8_e4m3fn_x4
E2M1 = mybir.dt.float4_e2m1fn_x4
MULT = mybir.AluOpType.mult

P = 128
PASSES = K // 512
HALF = S // 2
NC = 512
CHUNKS = M // NC
JT = S // P


def interleave(copy, out, in_):
    copy(out=out.rearrange("p (c i) t -> p c t i", i=4), in_=in_.rearrange("p t (c i) -> p c t i", i=4))


def tile_list_hlora_tm_res_kernel(tc, xT, w4_words, w4_scales, down, up, wgt, prev, offs, out):
    nc = tc.nc
    scopy = nc.scalar.copy
    vcopy = nc.vector.tensor_copy
    with ExitStack() as ctx:
        sb = ctx.enter_context(tc.tile_pool(name="sb", bufs=1))
        ps = ctx.enter_context(tc.psum_pool(name="ps", bufs=8))

        lists = sb.tile([P, S // 16], U16, name="lists")
        w4s = sb.tile([P, PASSES, M], U8, name="w4s", align_bytes=64)
        nc.vector.memset(w4s[:].bitcast(I32), 0)
        w4 = sb.tile([P, PASSES, 2 * M], U8, name="w4", align_bytes=64)
        wg = sb.tile([P, S], F32, name="wg")
        planes, draw, uraw, pv = {}, {}, {}, {}

        def load_x(a, i):
            planes[a, i] = sb.tile([P, T], F32, name=f"x{a}{i}")
            rows = xT[512 * a : 512 * (a + 1), :].rearrange("(p i) t -> p i t", i=4)
            nc.sync.dma_start(out=planes[a, i][:], in_=rows[:, i, :])

        def load_down(a):
            draw[a] = sb.tile([P, 4, R], F32, name=f"draw{a}")
            nc.sync.dma_start(out=draw[a][:], in_=down[512 * a : 512 * (a + 1), :].rearrange("(p j) r -> p j r", j=4))

        def load_up(c):
            uraw[c] = sb.tile([P, 4, NC], F32, name=f"uraw{c}")
            nc.sync.dma_start(out=uraw[c][:], in_=up[:, NC * c : NC * (c + 1)].rearrange("(p j) n -> p j n", j=4))

        nc.sync.dma_start(lists[:], offs)
        load_x(0, 0)
        nc.sync.dma_start(out=wg[:], in_=wgt)
        for i in range(1, 4):
            load_x(0, i)
        for i in range(4):
            load_x(1, i)
        for r in range(4):
            nc.sync.dma_start(
                out=w4s[r:P:32, :, :].bitcast(I32),
                in_=w4_scales.bitcast(I32).rearrange("a (q r) n -> r q a n", r=4)[r],
            )
        nc.sync.dma_start(out=w4[:].bitcast(I32), in_=w4_words.bitcast(I32).rearrange("a p n -> p a n"))
        load_down(0)
        load_down(1)
        for c in range(CHUNKS):
            load_up(c)
        for j in range(JT):
            pv[j] = sb.tile([P, M], F32, name=f"prev{j}")
            nc.sync.dma_start(out=pv[j][:], in_=prev[P * j : P * (j + 1), :])

        xc, xs, gath, xb = {}, {}, {}, {}
        for a in range(PASSES):
            xc[a] = sb.tile([P, S], U32, name=f"xc{a}", align_bytes=64)
            xs[a] = sb.tile([P, S], U8, name=f"xs{a}", align_bytes=64)
            for h in range(2):
                gath[a, h] = sb.tile([P, 4, HALF], F32, name=f"g{a}{h}")
                xb[a, h] = sb.tile([P, HALF, 4], BF16, name=f"xb{a}{h}", align_bytes=64)

        def gather(a, i, h):
            nc.vector.tensor_tensor(
                gath[a, h][:, i, :],
                planes[a, i][:].indirect(lists[:, h * HALF // 16 : (h + 1) * HALF // 16]),
                wg[:, h * HALF : (h + 1) * HALF],
                MULT,
            )

        def quantize_x(a, h):
            cols = slice(h * HALF, (h + 1) * HALF)
            nc.vector.quantize_mx(
                out=xc[a][:, cols].bitcast(E4M3), scales=xs[a][:, cols], in_=xb[a, h][:].rearrange("p j t -> p (j t)")
            )

        dc, ds, db = {}, {}, {}
        for a in range(PASSES):
            db[a] = sb.tile([P, R, 4], BF16, name=f"db{a}", align_bytes=64)
            dc[a] = sb.tile([P, R], U32, name=f"dc{a}", align_bytes=64)
            ds[a] = sb.tile([P, R], U8, name=f"ds{a}", align_bytes=64)

        def cast_down(copy, a, lo, hi):
            copy(
                out=db[a][:].rearrange("p (t m) j -> p m t j", t=4)[:, lo:hi],
                in_=draw[a][:].rearrange("p j (m t) -> p m t j", t=4)[:, lo:hi],
            )

        def quantize_down(a):
            nc.vector.quantize_mx(
                out=dc[a][:].bitcast(E4M3), scales=ds[a][:], in_=db[a][:].rearrange("p r j -> p (r j)")
            )

        ub, uc, us = [], [], []
        for c in range(CHUNKS):
            ub.append(sb.tile([P, NC, 4], BF16, name=f"ub{c}", align_bytes=64))
            uc.append(sb.tile([P, NC], U32, name=f"uc{c}", align_bytes=64))
            us.append(sb.tile([P, NC], U8, name=f"us{c}", align_bytes=64))

        def cast_up(copy, c, lo, hi):
            interleave(copy, ub[c][:, lo:hi, :], uraw[c][:, :, lo:hi])

        def quantize_up(c):
            nc.vector.quantize_mx(out=uc[c][:].bitcast(E4M3), scales=us[c][:], in_=ub[c][:].rearrange("p n j -> p (n j)"))

        for i in range(4):
            for h in range(2):
                gather(0, i, h)
        for h in range(2):
            interleave(scopy, xb[0, h][:], gath[0, h][:])
        for i in range(4):
            for h in range(2):
                gather(1, i, h)
            if i in (1, 2):
                quantize_x(0, i - 1)
        interleave(scopy, xb[1, 0][:], gath[1, 0][:])
        interleave(vcopy, xb[1, 1][:], gath[1, 1][:])
        cast_down(scopy, 0, 0, P)
        cast_down(vcopy, 1, 0, P)
        quantize_x(1, 0)
        quantize_x(1, 1)
        quantize_down(0)
        quantize_down(1)

        acc = {}

        def base(j, c):
            acc[j, c] = ps.tile([P, NC], F32, name=f"acc{j}{c}", tag="bank")
            for a in range(PASSES):
                nc.tensor.matmul_mx(
                    out=acc[j, c][:],
                    lhsT=xc[a][:, P * j : P * (j + 1)].bitcast(E4M3),
                    lhsT_scale=xs[a][:, P * j : P * (j + 1)],
                    rhs=w4[:, a, 2 * NC * c : 2 * NC * (c + 1)].bitcast(E2M1),
                    rhs_scale=w4s[:, a, NC * c : NC * (c + 1)],
                    start=(a == 0),
                    stop=False,
                )

        for j in range(2):
            for c in range(CHUNKS):
                base(j, c)

        hc = sb.tile([P, S], U32, name="hc", align_bytes=64)
        hs = sb.tile([P, S], U8, name="hs", align_bytes=64)
        for j in range(JT):
            cols = slice(P * j, P * (j + 1))
            bank = ps.tile([P, 4, P], F32, name=f"h{j}", tag="bank")
            for t in range(4):
                for a in range(PASSES):
                    nc.tensor.matmul_mx(
                        out=bank[:, t, :],
                        lhsT=dc[a][:, P * t : P * (t + 1)].bitcast(E4M3),
                        lhsT_scale=ds[a][:, P * t : P * (t + 1)],
                        rhs=xc[a][:, cols].bitcast(E4M3),
                        rhs_scale=xs[a][:, cols],
                        start=(a == 0),
                        stop=(a == PASSES - 1),
                    )
            hb = sb.tile([P, P, 4], BF16, name=f"hb{j}", align_bytes=64)
            scopy(out=hb[:], in_=bank[:].rearrange("p t j -> p j t"))
            nc.vector.quantize_mx(
                out=hc[:, cols].bitcast(E4M3), scales=hs[:, cols], in_=hb[:].rearrange("p j t -> p (j t)")
            )

        cast_up(scopy, 0, 0, NC)
        cast_up(vcopy, 1, 0, NC)
        quantize_up(0)
        cast_up(scopy, 2, 0, NC // 2)
        cast_up(vcopy, 2, NC // 2, NC)
        quantize_up(1)
        quantize_up(2)

        base(2, 0)
        base(2, 1)

        def finish(j, c, res):
            if (j, c) not in acc:
                base(j, c)
            nc.tensor.matmul_mx(
                out=acc[j, c][:],
                lhsT=hc[:, P * j : P * (j + 1)].bitcast(E4M3),
                lhsT_scale=hs[:, P * j : P * (j + 1)],
                rhs=uc[c][:].bitcast(E4M3),
                rhs_scale=us[c][:],
                start=False,
                stop=True,
            )
            residual = pv[j][:, NC * c : NC * (c + 1)]
            if (j, c) in ((1, 1), (2, 1), (3, 0)):
                y = sb.tile([P, NC], F32, name=f"y{j}")
                scopy(out=y[:], in_=acc[j, c][:])
                nc.gpsimd.tensor_tensor(out=res, in0=y[:], in1=residual, op=mybir.AluOpType.add)
            else:
                nc.vector.tensor_add(out=res, in0=acc[j, c][:], in1=residual)

        SPLIT = 2 * NC
        for j in range(2):
            left = sb.tile([P, SPLIT], F32, name=f"left{j}")
            for c in range(2):
                finish(j, c, left[:, NC * c : NC * (c + 1)])
            nc.sync.dma_start(out=out[P * j : P * (j + 1), :SPLIT], in_=left[:])
        right = sb.tile([P, 2, NC], F32, name="right")
        for j in range(2):
            finish(j, 2, right[:, j, :])
        nc.sync.dma_start(out=out[: 2 * P, SPLIT:].rearrange("(j p) n -> p j n", p=P), in_=right[:])
        for j in (2, 3):
            res = sb.tile([P, M], F32, name=f"res{j}")
            for c in range(CHUNKS):
                finish(j, c, res[:, NC * c : NC * (c + 1)])
            nc.sync.dma_start(out=out[P * j : P * (j + 1), :], in_=res[:])
